import numpy as np, ml_dtypes
CORES = [52,68,84,180,196,212,308,324,340]
N = 9
KB, QP = 4, 128
ROOT = 0
def setup_inputs(rng):
    q = rng.standard_normal((N, 128, QP), dtype=np.float32) / 4; k = rng.standard_normal((N, 128, KB * 128), dtype=np.float32)
    a = 2 * np.pi * rng.random((N, QP)); s = 400 * rng.random((N, QP)) ** 1.5; q[:, 0, :] = s * np.cos(a); q[:, 1, :] = s * np.sin(a); q[:, 2, :] = 150 * rng.standard_normal((N, QP)); k[:, 2, :] = 1 + k[:, 2, :] / 50
    a = (2 * np.pi * rng.random() + np.pi / 2 * (rng.permutation(N).reshape(N, 1, 1) + 0.5) / N - 0.5 + (np.arange(KB).reshape(1, KB, 1) + rng.random((N, KB, 128))) / KB).reshape(N, KB * 128); k[:, 0, :] = np.cos(a); k[:, 1, :] = np.sin(a)
    for t in range(0, QP, 2):
        j, i = (t // 2) % N, rng.integers(KB * 128); q[ROOT, :2, t] = s[ROOT, t] * k[j, :2, i]; q[ROOT, 3:, t] += k[j, 3:, i] / 8
    return {"q": q.astype(ml_dtypes.bfloat16), "k": k.astype(ml_dtypes.bfloat16), "v": rng.standard_normal((N, 128, KB * 128), dtype=np.float32).astype(ml_dtypes.bfloat16)}
def setup_inputs_big(rng):
    d = setup_inputs(rng)
    for k in ("v",): d[k] = (d[k].astype(np.float32) * 1048576.0).astype(d[k].dtype)
    return d
def setup_inputs_small(rng):
    d = setup_inputs(rng)
    for k in ("v",): d[k] = (d[k].astype(np.float32) * (1 / 1048576.0)).astype(d[k].dtype)
    return d
def reference(q, k, v):
    Q, K, V = q.astype(np.float64), k.astype(np.float64), v.astype(np.float64)
    y = np.full((N, QP, 128), np.nan)
    for r in [ROOT]:
        js = list(range(N))
        S = np.concatenate([K[j].T @ Q[r] for j in js], axis=0)
        P = np.exp(S - S.max(axis=0)); P = P / P.sum(axis=0)
        y[r] = P.T @ np.concatenate([V[j][:, 128 * b:128 * b + 128] for j in js for b in range(KB)], axis=0)
    return {"y": y.astype(ml_dtypes.bfloat16)}

@@ -1,0 +1,192 @@
+from concourse.bass import DstId, RemoteDMATransfer
+from concourse.mybir import AluOpType, AxisListType, ActivationFunctionType
+
+KB = 4
+VW = 136
+OW = 129
+NP = 9
+
+SCRATCH = {
+    "q_sb": ("sbuf", [128, 128], "bfloat16"),
+    "k_sb": ("sbuf", [128, 512], "bfloat16"),
+    "vaug": ("sbuf", [128, KB, VW], "bfloat16"),
+    "zeros": ("sbuf", [128, 128], "bfloat16"),
+    "ones": ("sbuf", [128, 128], "bfloat16"),
+    "ident": ("sbuf", [128, 128], "bfloat16"),
+    "mx": ("sbuf", [128, 4], "float32"),
+    "nland": ("sbuf", [128, 16], "bfloat16"),
+    "pw": ("sbuf", [128, 512], "bfloat16"),
+    "pt": ("sbuf", [128, 512], "bfloat16"),
+    "oland": ("sbuf", [128, NP, VW], "bfloat16"),
+    "mn": ("sbuf", [128, 1], "float32"),
+    "ew": ("sbuf", [128, 16], "bfloat16"),
+    "dg": ("sbuf", [128, NP * 128], "bfloat16"),
+    "rc": ("sbuf", [128, 1], "float32"),
+    "ysb": ("sbuf", [128, 128], "bfloat16"),
+    "S0": ("psum", [128, 512], "float32"),
+    "S1": ("psum", [128, 512], "float32"),
+    "S2": ("psum", [128, 512], "float32"),
+    "S3": ("psum", [128, 512], "float32"),
+    "O": ("psum", [128, 512], "float32"),
+    "Y": ("psum", [128, 512], "float32"),
+}
+SEMAPHORES = (["qin", "kin", "vin", "pad", "zz", "one", "idn", "r", "nm", "pv", "od", "snt",
+               "na", "mn", "ee", "yy", "rcp", "ys", "st"]
+              + ["s%d" % b for b in range(KB)] + ["p%d" % b for b in range(KB)]
+              + ["t%d" % b for b in range(KB)] + ["c%d" % b for b in range(KB)]
+              + ["oa%d" % j for j in range(NP)] + ["d%d" % j for j in range(NP)])
+
+
+def _engines(mask):
+    return bin(mask).count("1")
+
+
+def _plan(T, topo):
+    ranks = list(T.cores)
+    root = ranks[T.root]
+    near = [c for c in ranks if c != root and topo.may_write(root, c) and topo.may_write(c, root)]
+    far = [c for c in ranks if c != root and c not in near]
+    stand = {}
+    for s in far:
+        gate = [w for w in near if topo.chip(w) == topo.chip(s) and topo.may_write(s, w)
+                and topo.rack(topo.host(w)) != topo.rack(topo.host(s))][0]
+        w = topo.CORES_PER_CHIP
+        stand[s] = [c for c in range(max(0, gate - w), gate + w)
+                    if topo.host(c) == topo.host(gate) and topo.chip(c) == topo.chip(gate) and c not in ranks
+                    and topo.die(c) != topo.die(gate)
+                    and topo.may_write(s, c) and topo.may_write(root, c) and topo.may_write(c, root)][0]
+    return root, near + [stand[s] for s in far], stand
+
+
+def rank_program(g, core, T, topo):
+    root, workers, stand = _plan(T, topo)
+    sem = T.sem
+    own = NP - 1
+
+    if core in stand:
+        d = stand[core]
+        rid, pid = topo.addr(d, core)
+        m = topo.mask(core, d)
+        for b in range(KB):
+            g.vector.memset(T.vaug[:, b, 128:VW], 1.0).then_inc(sem.pad, 1)
+        g.sync.dma_start(T.k_sb[:, :], T.k[:, :]).then_inc(sem.kin, 16)
+        g.sync.dma_start(T.vaug[:, :, 0:128], T.v[:, :]).then_inc(sem.vin, 16)
+        g.wait_ge(sem.kin, 16)
+        g.remote_dma(T.k_sb[:, :], T.k_sb[:, :], sem.kin, sem.snt, pid, rid, m)
+        g.wait_ge(sem.vin, 16)
+        g.wait_ge(sem.pad, KB)
+        g.remote_dma(T.vaug[:, :, :], T.vaug[:, :, :], sem.vin, sem.snt, pid, rid, m)
+        g.wait_ge(sem.snt, 2 * _engines(m))
+        return
+    if core != root and core not in workers:
+        return
+
+    is_root = core == root
+    local_kv = T.rank_of(core) is not None
+    S = [T.S0, T.S1, T.S2, T.S3]
+    qmask = topo.mask(root, workers[0])
+    for d in workers:
+        qmask &= topo.mask(root, d)
+
+    if is_root:
+        g.sync.dma_start(T.q_sb[:, :], T.q[:, :]).then_inc(sem.qin, 16)
+    if local_kv:
+        g.sync.dma_start(T.k_sb[:, :], T.k[:, :]).then_inc(sem.kin, 16)
+        g.sync.dma_start(T.vaug[:, :, 0:128], T.v[:, :]).then_inc(sem.vin, 16)
+    q_here = 16 if is_root else _engines(qmask)
+    if local_kv:
+        kv_here = 16
+    else:
+        src = [s for s in stand if stand[s] == core][0]
+        kv_here = _engines(topo.mask(src, core))
+
+    if is_root:
+        g.wait_ge(sem.qin, 16)
+        ids = []
+        for d in workers:
+            rid, pid = topo.addr(d, core)
+            ids.append(DstId(rid=rid, pnc=pid))
+        g.remote_dma_fused([RemoteDMATransfer(dst_ids=ids, dma_engine_mask=qmask, remote_sem=sem.qin,
+                                              srcs=[T.q_sb[:, :]], dsts=[T.q_sb[:, :] for _ in workers], alu_op=0)],
+                           local_sem=sem.snt)
+    g.vector.memset(T.zeros[:, :], 0.0).then_inc(sem.zz, 1)
+    if local_kv:
+        for b in range(KB):
+            g.vector.memset(T.vaug[:, b, 128:VW], 1.0).then_inc(sem.pad, 1)
+    g.scalar.wait_ge(sem.zz, 1)
+    g.scalar.activation(T.ones[:, :], T.zeros[:, :], ActivationFunctionType.Exp).then_inc(sem.one, 1)
+    g.wait_ge(sem.one, 1)
+    g.affine_select(T.ident[:, :], T.ones[:, :], [[-1, 128]], AluOpType.is_equal, 0.0, 0, 1).then_inc(sem.idn, 1)
+
+    g.tensor.wait_ge(sem.qin, q_here)
+    g.tensor.wait_ge(sem.kin, kv_here)
+    for b in range(KB):
+        g.tensor.matmul(S[b][:, 0:128], T.q_sb[:, :], T.k_sb[:, 128 * b:128 * b + 128], True, True).then_inc(sem["s%d" % b], 1)
+    for b in range(KB):
+        g.vector.wait_ge(sem["s%d" % b], 1)
+        g.vector.tensor_reduce(T.mx[:, b:b + 1], S[b][:, 0:128], AxisListType.X, AluOpType.max).then_inc(sem.r, 1)
+    g.vector.wait_ge(sem.r, KB)
+    g.vector.tensor_reduce(T.nland[:, own:own + 1], T.mx[:, 0:KB], AxisListType.X, AluOpType.max,
+                           negate=True).then_inc(sem.nm, 1)
+    g.scalar.wait_ge(sem.nm, 1)
+    for b in range(KB):
+        g.scalar.activation(T.pw[:, 128 * b:128 * b + 128], S[b][:, 0:128], ActivationFunctionType.Exp,
+                            bias=T.nland[:, own:own + 1], scale=1.0).then_inc(sem["p%d" % b], 1)
+    g.tensor.wait_ge(sem.idn, 1)
+    for b in range(KB):
+        g.tensor.wait_ge(sem["p%d" % b], 1)
+        g.tensor.matmul(S[b][:, 128:256], T.pw[:, 128 * b:128 * b + 128], T.ident[:, :], True, True).then_inc(sem["t%d" % b], 1)
+    for b in range(KB):
+        g.vector.wait_ge(sem["t%d" % b], 1)
+        g.vector.tensor_copy(T.pt[:, 128 * b:128 * b + 128], S[b][:, 128:256]).then_inc(sem["c%d" % b], 1)
+    g.tensor.wait_ge(sem.vin, kv_here)
+    if local_kv:
+        g.tensor.wait_ge(sem.pad, KB)
+    for b in range(KB):
+        g.tensor.wait_ge(sem["c%d" % b], 1)
+        mm = g.tensor.matmul(T.O[:, 0:OW], T.pt[:, 128 * b:128 * b + 128], T.vaug[:, b, 0:OW], b == 0, b == KB - 1)
+        if b == KB - 1:
+            mm.then_inc(sem.pv, 1)
+    g.vector.wait_ge(sem.pv, 1)
+    g.vector.tensor_copy(T.oland[:, own, 0:OW], T.O[:, 0:OW]).then_inc(sem.od, 1)
+
+    if not is_root:
+        j = workers.index(core)
+        rid, pid = topo.addr(root, core)
+        m = topo.mask(core, root)
+        g.wait_ge(sem.nm, 1)
+        g.remote_dma(T.nland[:, j:j + 1], T.nland[:, own:own + 1], sem.na, sem.snt, pid, rid, m)
+        g.wait_ge(sem.od, 1)
+        g.remote_dma(T.oland[:, j, 0:OW], T.oland[:, own, 0:OW], sem["oa%d" % j], sem.snt, pid, rid, m)
+        g.wait_ge(sem.snt, 2 * _engines(m))
+        return
+
+    g.vector.wait_ge(sem.na, sum(_engines(topo.mask(w, root)) for w in workers))
+    g.vector.wait_ge(sem.nm, 1)
+    g.vector.tensor_reduce(T.mn[:, 0:1], T.nland[:, 0:NP], AxisListType.X, AluOpType.min).then_inc(sem.mn, 1)
+    g.scalar.wait_ge(sem.mn, 1)
+    g.scalar.activation(T.ew[:, 0:NP], T.nland[:, 0:NP], ActivationFunctionType.Exp,
+                        bias=T.mn[:, 0:1], scale=-1.0).then_inc(sem.ee, 1)
+    order = [own] + list(range(len(workers)))
+    g.vector.wait_ge(sem.ee, 1)
+    g.vector.wait_ge(sem.idn, 1)
+    for j in order:
+        g.vector.tensor_scalar(T.dg[:, 128 * j:128 * j + 128], T.ident[:, :], T.ew[:, j:j + 1], None,
+                               AluOpType.mult).then_inc(sem["d%d" % j], 1)
+    for i, j in enumerate(order):
+        g.tensor.wait_ge(sem["d%d" % j], 1)
+        if j == own:
+            g.tensor.wait_ge(sem.od, 1)
+        else:
+            g.tensor.wait_ge(sem["oa%d" % j], _engines(topo.mask(workers[j], root)))
+        mm = g.tensor.matmul(T.Y[:, 0:OW], T.dg[:, 128 * j:128 * j + 128], T.oland[:, j, 0:OW], i == 0, i == len(order) - 1)
+        if i == len(order) - 1:
+            mm.then_inc(sem.yy, 1)
+    g.vector.wait_ge(sem.yy, 1)
+    g.vector.reciprocal(T.rc[:, 0:1], T.Y[:, 128:129]).then_inc(sem.rcp, 1)
+    g.vector.wait_ge(sem.rcp, 1)
+    g.vector.tensor_scalar(T.ysb[:, :], T.Y[:, 0:128], T.rc[:, 0:1], None, AluOpType.mult).then_inc(sem.ys, 1)
+    g.sync.wait_ge(sem.ys, 1)
+    g.sync.dma_start(T.y[:, :], T.ysb[:, :]).then_inc(sem.st, 16)
+    g.sync.wait_ge(sem.st, 16)
+    g.wait_ge(sem.snt, _engines(qmask))

@@ -8,16 +8,18 @@ NP = 9
 
 SCRATCH = {
     "q_sb": ("sbuf", [128, 128], "bfloat16"),
-    "k_sb": ("sbuf", [128, 512], "bfloat16"),
-    "vaug": ("sbuf", [128, KB, VW], "bfloat16"),
+    "k_sb0": ("sbuf", [128, 512], "bfloat16"),
+    "k_sb1": ("sbuf", [128, 512], "bfloat16"),
+    "vaug0": ("sbuf", [128, KB, VW], "bfloat16"),
+    "vaug1": ("sbuf", [128, KB, VW], "bfloat16"),
     "zeros": ("sbuf", [128, 128], "bfloat16"),
     "ones": ("sbuf", [128, 128], "bfloat16"),
     "ident": ("sbuf", [128, 128], "bfloat16"),
-    "mx": ("sbuf", [128, 4], "float32"),
+    "mx": ("sbuf", [128, 8], "float32"),
     "nland": ("sbuf", [128, 16], "bfloat16"),
-    "pw": ("sbuf", [128, 512], "bfloat16"),
-    "pt": ("sbuf", [128, 512], "bfloat16"),
-    "oland": ("sbuf", [128, NP, VW], "bfloat16"),
+    "pw": ("sbuf", [128, 1024], "bfloat16"),
+    "pt": ("sbuf", [128, 1024], "bfloat16"),
+    "oland": ("sbuf", [128, NP + 1, VW], "bfloat16"),
     "mn": ("sbuf", [128, 1], "float32"),
     "ew": ("sbuf", [128, 16], "bfloat16"),
     "dg": ("sbuf", [128, NP * 128], "bfloat16"),
@@ -30,10 +32,10 @@ SCRATCH = {
     "O": ("psum", [128, 512], "float32"),
     "Y": ("psum", [128, 512], "float32"),
 }
-SEMAPHORES = (["qin", "kin", "vin", "pad", "zz", "one", "idn", "r", "nm", "pv", "od", "snt",
-               "na", "mn", "ee", "yy", "rcp", "ys", "st"]
-              + ["s%d" % b for b in range(KB)] + ["p%d" % b for b in range(KB)]
-              + ["t%d" % b for b in range(KB)] + ["c%d" % b for b in range(KB)]
+SEMAPHORES = (["qin", "kin", "vin", "pin", "pad", "zz", "one", "idn", "snt", "na", "mn", "ee", "yy", "rcp", "ys", "st"]
+              + ["%s%d" % (n, i) for i in range(2) for n in ("r", "nm", "pv", "od")]
+              + ["%s%d%d" % (n, i, b) for i in range(2) for n in "sptc" for b in range(KB)]
+              + ["kb%d" % b for b in range(KB)] + ["vb%d" % b for b in range(KB)]
               + ["oa%d" % j for j in range(NP)] + ["d%d" % j for j in range(NP)])
 
 
@@ -41,133 +43,190 @@ def _engines(mask):
     return bin(mask).count("1")
 
 
+def _bits(mask):
+    return [1 << e for e in range(mask.bit_length()) if (mask >> e) & 1]
+
+
 def _plan(T, topo):
     ranks = list(T.cores)
     root = ranks[T.root]
     near = [c for c in ranks if c != root and topo.may_write(root, c) and topo.may_write(c, root)]
     far = [c for c in ranks if c != root and c not in near]
-    stand = {}
+    gate, deal = {}, {}
     for s in far:
-        gate = [w for w in near if topo.chip(w) == topo.chip(s) and topo.may_write(s, w)
-                and topo.rack(topo.host(w)) != topo.rack(topo.host(s))][0]
+        gate[s] = [w for w in near if topo.chip(w) == topo.chip(s) and topo.may_write(s, w)
+                   and topo.rack(topo.host(w)) != topo.rack(topo.host(s))][0]
         w = topo.CORES_PER_CHIP
-        stand[s] = [c for c in range(max(0, gate - w), gate + w)
-                    if topo.host(c) == topo.host(gate) and topo.chip(c) == topo.chip(gate) and c not in ranks
-                    and topo.die(c) != topo.die(gate)
-                    and topo.may_write(s, c) and topo.may_write(root, c) and topo.may_write(c, root)][0]
-    return root, near + [stand[s] for s in far], stand
+        chipc = [c for c in range(max(0, s - w), s + w) if topo.host(c) == topo.host(s) and topo.chip(c) == topo.chip(s)
+                 and topo.may_write(c, gate[s])]
+        par = chipc.index(s) % 2
+        kc = [s] + [c for i, c in enumerate(chipc) if i % 2 == par and c != s]
+        vc = [c for i, c in enumerate(chipc) if i % 2 != par]
+        deal[s] = (kc[:KB], vc[:KB])
+    gates = [gate[s] for s in far]
+    return root, gates + [c for c in near if c not in gates], gate, deal
 
 
 def rank_program(g, core, T, topo):
-    root, workers, stand = _plan(T, topo)
+    root, near, gate, deal = _plan(T, topo)
     sem = T.sem
-    own = NP - 1
+    far = list(gate)
 
-    if core in stand:
-        d = stand[core]
-        rid, pid = topo.addr(d, core)
-        m = topo.mask(core, d)
+    if core in gate:
+        d = gate[core]
+        kc, vc = deal[core]
+        off = topo.mask(core, d)
+        on = _bits(topo.mask(core, kc[1]))
+        up = [e for e in on if not e & off]
         for b in range(KB):
-            g.vector.memset(T.vaug[:, b, 128:VW], 1.0).then_inc(sem.pad, 1)
-        g.sync.dma_start(T.k_sb[:, :], T.k[:, :]).then_inc(sem.kin, 16)
-        g.sync.dma_start(T.vaug[:, :, 0:128], T.v[:, :]).then_inc(sem.vin, 16)
+            g.vector.memset(T.vaug0[:, b, 128:VW], 1.0).then_inc(sem.pad, 1)
+        g.sync.dma_start(T.k_sb0[:, :], T.k[:, :]).then_inc(sem.kin, 16)
+        g.sync.dma_start(T.vaug0[:, :, 0:128], T.v[:, :]).then_inc(sem.vin, 16)
+        h, qr = len(up) // 2, len(up) // 4
+        km = [None, sum(up[0:h]), sum(up[h:h + qr]), sum(up[h + qr:h + 2 * qr])]
+        tr = []
+        for b in range(1, KB):
+            rid, pid = topo.addr(kc[b], core)
+            tr.append(RemoteDMATransfer(dst_ids=[DstId(rid=rid, pnc=pid)], dma_engine_mask=km[b], remote_sem=sem.pin,
+                                        src=T.k_sb0[:, 128 * b:128 * b + 128], dst=T.k_sb0[:, 128 * b:128 * b + 128]))
         g.wait_ge(sem.kin, 16)
-        g.remote_dma(T.k_sb[:, :], T.k_sb[:, :], sem.kin, sem.snt, pid, rid, m)
+        g.remote_dma_fused(tr, local_sem=sem.snt)
+        rid, pid = topo.addr(d, core)
+        g.remote_dma(T.k_sb1[:, 0:128], T.k_sb0[:, 0:128], sem.kb0, sem.snt, pid, rid, off)
+        n4 = len(on) // KB
+        tr = []
+        for b in range(KB):
+            rid, pid = topo.addr(vc[b], core)
+            tr.append(RemoteDMATransfer(dst_ids=[DstId(rid=rid, pnc=pid)], dma_engine_mask=sum(on[n4 * b:n4 * b + n4]),
+                                        remote_sem=sem.pin, src=T.vaug0[:, b, :], dst=T.vaug0[:, b, :]))
         g.wait_ge(sem.vin, 16)
         g.wait_ge(sem.pad, KB)
-        g.remote_dma(T.vaug[:, :, :], T.vaug[:, :, :], sem.vin, sem.snt, pid, rid, m)
-        g.wait_ge(sem.snt, 2 * _engines(m))
+        g.remote_dma_fused(tr, local_sem=sem.snt)
+        g.wait_ge(sem.snt, sum(_engines(x) for x in km[1:]) + _engines(off) + n4 * KB)
         return
-    if core != root and core not in workers:
+    for s in far:
+        kc, vc = deal[s]
+        if core in kc or core in vc:
+            d = gate[s]
+            rid, pid = topo.addr(d, core)
+            m = topo.mask(core, d)
+            on = _bits(topo.mask(s, core))
+            up = [e for e in on if not e & topo.mask(s, d)]
+            if core in kc:
+                b = kc.index(core)
+                g.wait_ge(sem.pin, len(up) // 2 if b == 1 else len(up) // 4)
+                g.remote_dma(T.k_sb1[:, 128 * b:128 * b + 128], T.k_sb0[:, 128 * b:128 * b + 128], sem["kb%d" % b], sem.snt,
+                             pid, rid, m)
+            else:
+                b = vc.index(core)
+                g.wait_ge(sem.pin, len(on) // KB)
+                g.remote_dma(T.vaug1[:, b, :], T.vaug0[:, b, :], sem["vb%d" % b], sem.snt, pid, rid, m)
+            g.wait_ge(sem.snt, _engines(m))
+            return
+    if core != root and core not in near:
         return
 
     is_root = core == root
-    local_kv = T.rank_of(core) is not None
     S = [T.S0, T.S1, T.S2, T.S3]
-    qmask = topo.mask(root, workers[0])
-    for d in workers:
+    qmask = topo.mask(root, near[0])
+    for d in near:
         qmask &= topo.mask(root, d)
 
     if is_root:
         g.sync.dma_start(T.q_sb[:, :], T.q[:, :]).then_inc(sem.qin, 16)
-    if local_kv:
-        g.sync.dma_start(T.k_sb[:, :], T.k[:, :]).then_inc(sem.kin, 16)
-        g.sync.dma_start(T.vaug[:, :, 0:128], T.v[:, :]).then_inc(sem.vin, 16)
-    q_here = 16 if is_root else _engines(qmask)
-    if local_kv:
-        kv_here = 16
-    else:
-        src = [s for s in stand if stand[s] == core][0]
-        kv_here = _engines(topo.mask(src, core))
+    g.sync.dma_start(T.k_sb0[:, :], T.k[:, :]).then_inc(sem.kin, 16)
+    g.sync.dma_start(T.vaug0[:, :, 0:128], T.v[:, :]).then_inc(sem.vin, 16)
 
     if is_root:
         g.wait_ge(sem.qin, 16)
         ids = []
-        for d in workers:
+        for d in near:
             rid, pid = topo.addr(d, core)
             ids.append(DstId(rid=rid, pnc=pid))
         g.remote_dma_fused([RemoteDMATransfer(dst_ids=ids, dma_engine_mask=qmask, remote_sem=sem.qin,
-                                              srcs=[T.q_sb[:, :]], dsts=[T.q_sb[:, :] for _ in workers], alu_op=0)],
+                                              srcs=[T.q_sb[:, :]], dsts=[T.q_sb[:, :] for _ in near], alu_op=0)],
                            local_sem=sem.snt)
     g.vector.memset(T.zeros[:, :], 0.0).then_inc(sem.zz, 1)
-    if local_kv:
-        for b in range(KB):
-            g.vector.memset(T.vaug[:, b, 128:VW], 1.0).then_inc(sem.pad, 1)
+    for b in range(KB):
+        g.vector.memset(T.vaug0[:, b, 128:VW], 1.0).then_inc(sem.pad, 1)
     g.scalar.wait_ge(sem.zz, 1)
     g.scalar.activation(T.ones[:, :], T.zeros[:, :], ActivationFunctionType.Exp).then_inc(sem.one, 1)
     g.wait_ge(sem.one, 1)
     g.affine_select(T.ident[:, :], T.ones[:, :], [[-1, 128]], AluOpType.is_equal, 0.0, 0, 1).then_inc(sem.idn, 1)
-
-    g.tensor.wait_ge(sem.qin, q_here)
-    g.tensor.wait_ge(sem.kin, kv_here)
-    for b in range(KB):
-        g.tensor.matmul(S[b][:, 0:128], T.q_sb[:, :], T.k_sb[:, 128 * b:128 * b + 128], True, True).then_inc(sem["s%d" % b], 1)
-    for b in range(KB):
-        g.vector.wait_ge(sem["s%d" % b], 1)
-        g.vector.tensor_reduce(T.mx[:, b:b + 1], S[b][:, 0:128], AxisListType.X, AluOpType.max).then_inc(sem.r, 1)
-    g.vector.wait_ge(sem.r, KB)
-    g.vector.tensor_reduce(T.nland[:, own:own + 1], T.mx[:, 0:KB], AxisListType.X, AluOpType.max,
-                           negate=True).then_inc(sem.nm, 1)
-    g.scalar.wait_ge(sem.nm, 1)
-    for b in range(KB):
-        g.scalar.activation(T.pw[:, 128 * b:128 * b + 128], S[b][:, 0:128], ActivationFunctionType.Exp,
-                            bias=T.nland[:, own:own + 1], scale=1.0).then_inc(sem["p%d" % b], 1)
+    g.tensor.wait_ge(sem.qin, 16 if is_root else _engines(qmask))
     g.tensor.wait_ge(sem.idn, 1)
-    for b in range(KB):
-        g.tensor.wait_ge(sem["p%d" % b], 1)
-        g.tensor.matmul(S[b][:, 128:256], T.pw[:, 128 * b:128 * b + 128], T.ident[:, :], True, True).then_inc(sem["t%d" % b], 1)
-    for b in range(KB):
-        g.vector.wait_ge(sem["t%d" % b], 1)
-        g.vector.tensor_copy(T.pt[:, 128 * b:128 * b + 128], S[b][:, 128:256]).then_inc(sem["c%d" % b], 1)
-    g.tensor.wait_ge(sem.vin, kv_here)
-    if local_kv:
-        g.tensor.wait_ge(sem.pad, KB)
-    for b in range(KB):
-        g.tensor.wait_ge(sem["c%d" % b], 1)
-        mm = g.tensor.matmul(T.O[:, 0:OW], T.pt[:, 128 * b:128 * b + 128], T.vaug[:, b, 0:OW], b == 0, b == KB - 1)
-        if b == KB - 1:
-            mm.then_inc(sem.pv, 1)
-    g.vector.wait_ge(sem.pv, 1)
-    g.vector.tensor_copy(T.oland[:, own, 0:OW], T.O[:, 0:OW]).then_inc(sem.od, 1)
+    g.tensor.wait_ge(sem.pad, KB)
 
+    groups = [(0, None if is_root else near.index(core), None)]
+    for s in far:
+        if gate[s] == core:
+            groups.append((1, len(near) + far.index(s), s))
     if not is_root:
-        j = workers.index(core)
         rid, pid = topo.addr(root, core)
         m = topo.mask(core, root)
-        g.wait_ge(sem.nm, 1)
-        g.remote_dma(T.nland[:, j:j + 1], T.nland[:, own:own + 1], sem.na, sem.snt, pid, rid, m)
-        g.wait_ge(sem.od, 1)
-        g.remote_dma(T.oland[:, j, 0:OW], T.oland[:, own, 0:OW], sem["oa%d" % j], sem.snt, pid, rid, m)
-        g.wait_ge(sem.snt, 2 * _engines(m))
+
+    for i, slot, s in groups:
+        k_sb, vaug = (T.k_sb0, T.vaug0) if i == 0 else (T.k_sb1, T.vaug1)
+        own = NP - 1 + i
+        c0 = 512 * i
+
+        def sm(n, b=None):
+            return sem["%s%d" % (n, i)] if b is None else sem["%s%d%d" % (n, i, b)]
+        for b in range(KB):
+            if s is None:
+                g.tensor.wait_ge(sem.kin, 16)
+            else:
+                g.tensor.wait_ge(sem["kb%d" % b], _engines(topo.mask(deal[s][0][b], core)))
+            g.tensor.matmul(S[b][:, 0:128], T.q_sb[:, :], k_sb[:, 128 * b:128 * b + 128], True, True).then_inc(sm("s", b), 1)
+        for b in range(KB):
+            g.vector.wait_ge(sm("s", b), 1)
+            g.vector.tensor_reduce(T.mx[:, 4 * i + b:4 * i + b + 1], S[b][:, 0:128], AxisListType.X,
+                                   AluOpType.max).then_inc(sm("r"), 1)
+        g.vector.wait_ge(sm("r"), KB)
+        g.vector.tensor_reduce(T.nland[:, own:own + 1], T.mx[:, 4 * i:4 * i + KB], AxisListType.X, AluOpType.max,
+                               negate=True).then_inc(sm("nm"), 1)
+        g.scalar.wait_ge(sm("nm"), 1)
+        for b in range(KB):
+            g.scalar.activation(T.pw[:, c0 + 128 * b:c0 + 128 * b + 128], S[b][:, 0:128], ActivationFunctionType.Exp,
+                                bias=T.nland[:, own:own + 1], scale=1.0).then_inc(sm("p", b), 1)
+        for b in range(KB):
+            g.tensor.wait_ge(sm("p", b), 1)
+            g.tensor.matmul(S[b][:, 128:256], T.pw[:, c0 + 128 * b:c0 + 128 * b + 128], T.ident[:, :], True,
+                            True).then_inc(sm("t", b), 1)
+        for b in range(KB):
+            g.vector.wait_ge(sm("t", b), 1)
+            g.vector.tensor_copy(T.pt[:, c0 + 128 * b:c0 + 128 * b + 128], S[b][:, 128:256]).then_inc(sm("c", b), 1)
+        if i > 0:
+            g.tensor.wait_ge(sem.od0, 1)
+        for b in range(KB):
+            if s is None:
+                g.tensor.wait_ge(sem.vin, 16)
+            else:
+                g.tensor.wait_ge(sem["vb%d" % b], _engines(topo.mask(deal[s][1][b], core)))
+            g.tensor.wait_ge(sm("c", b), 1)
+            mm = g.tensor.matmul(T.O[:, 0:OW], T.pt[:, c0 + 128 * b:c0 + 128 * b + 128], vaug[:, b, 0:OW], b == 0, b == KB - 1)
+            if b == KB - 1:
+                mm.then_inc(sm("pv"), 1)
+        g.vector.wait_ge(sm("pv"), 1)
+        g.vector.tensor_copy(T.oland[:, own, 0:OW], T.O[:, 0:OW]).then_inc(sm("od"), 1)
+        if not is_root:
+            g.wait_ge(sm("nm"), 1)
+            g.remote_dma(T.nland[:, slot:slot + 1], T.nland[:, own:own + 1], sem.na, sem.snt, pid, rid, m)
+            g.wait_ge(sm("od"), 1)
+            g.remote_dma(T.oland[:, slot, 0:OW], T.oland[:, own, 0:OW], sem["oa%d" % slot], sem.snt, pid, rid, m)
+    if not is_root:
+        g.wait_ge(sem.snt, 2 * len(groups) * _engines(m))
         return
 
-    g.vector.wait_ge(sem.na, sum(_engines(topo.mask(w, root)) for w in workers))
-    g.vector.wait_ge(sem.nm, 1)
+    own = NP - 1
+    sender = near + [gate[s] for s in far]
+    g.vector.wait_ge(sem.na, sum(_engines(topo.mask(w, root)) for w in sender))
+    g.vector.wait_ge(sem.nm0, 1)
     g.vector.tensor_reduce(T.mn[:, 0:1], T.nland[:, 0:NP], AxisListType.X, AluOpType.min).then_inc(sem.mn, 1)
     g.scalar.wait_ge(sem.mn, 1)
     g.scalar.activation(T.ew[:, 0:NP], T.nland[:, 0:NP], ActivationFunctionType.Exp,
                         bias=T.mn[:, 0:1], scale=-1.0).then_inc(sem.ee, 1)
-    order = [own] + list(range(len(workers)))
+    order = [own] + list(range(len(sender)))
     g.vector.wait_ge(sem.ee, 1)
     g.vector.wait_ge(sem.idn, 1)
     for j in order:
@@ -176,9 +235,9 @@ def rank_program(g, core, T, topo):
     for i, j in enumerate(order):
         g.tensor.wait_ge(sem["d%d" % j], 1)
         if j == own:
-            g.tensor.wait_ge(sem.od, 1)
+            g.tensor.wait_ge(sem.od0, 1)
         else:
-            g.tensor.wait_ge(sem["oa%d" % j], _engines(topo.mask(workers[j], root)))
+            g.tensor.wait_ge(sem["oa%d" % j], _engines(topo.mask(sender[j], root)))
         mm = g.tensor.matmul(T.Y[:, 0:OW], T.dg[:, 128 * j:128 * j + 128], T.oland[:, j, 0:OW], i == 0, i == len(order) - 1)
         if i == len(order) - 1:
             mm.then_inc(sem.yy, 1)

from concourse.bass import DstId, RemoteDMATransfer
from concourse.mybir import AluOpType, AxisListType, ActivationFunctionType

KB = 4
VW = 136
OW = 129
NP = 9

SCRATCH = {
    "q_sb": ("sbuf", [128, 128], "bfloat16"),
    "k_sb0": ("sbuf", [128, 512], "bfloat16"),
    "k_sb1": ("sbuf", [128, 512], "bfloat16"),
    "vaug0": ("sbuf", [128, KB, VW], "bfloat16"),
    "vaug1": ("sbuf", [128, KB, VW], "bfloat16"),
    "zeros": ("sbuf", [128, 128], "bfloat16"),
    "ones": ("sbuf", [128, 128], "bfloat16"),
    "ident": ("sbuf", [128, 128], "bfloat16"),
    "mx": ("sbuf", [128, 8], "float32"),
    "nland": ("sbuf", [128, 16], "bfloat16"),
    "pw": ("sbuf", [128, 1024], "bfloat16"),
    "pt": ("sbuf", [128, 1024], "bfloat16"),
    "oland": ("sbuf", [128, NP + 1, VW], "bfloat16"),
    "mn": ("sbuf", [128, 1], "float32"),
    "ew": ("sbuf", [128, 16], "bfloat16"),
    "dg": ("sbuf", [128, NP * 128], "bfloat16"),
    "rc": ("sbuf", [128, 1], "float32"),
    "ysb": ("sbuf", [128, 128], "bfloat16"),
    "S0": ("psum", [128, 512], "float32"),
    "S1": ("psum", [128, 512], "float32"),
    "S2": ("psum", [128, 512], "float32"),
    "S3": ("psum", [128, 512], "float32"),
    "O": ("psum", [128, 512], "float32"),
    "Y": ("psum", [128, 512], "float32"),
}
SEMAPHORES = (["qin", "kin", "vin", "pin", "pad", "zz", "one", "idn", "snt", "na", "mn", "ee", "yy", "rcp", "ys", "st"]
              + ["%s%d" % (n, i) for i in range(2) for n in ("r", "nm", "pv", "od")]
              + ["%s%d%d" % (n, i, b) for i in range(2) for n in "sptc" for b in range(KB)]
              + ["kb%d" % b for b in range(KB)] + ["vb%d" % b for b in range(KB)]
              + ["oa%d" % j for j in range(NP)] + ["d%d" % j for j in range(NP)])


def _engines(mask):
    return bin(mask).count("1")


def _bits(mask):
    return [1 << e for e in range(mask.bit_length()) if (mask >> e) & 1]


def _plan(T, topo):
    ranks = list(T.cores)
    root = ranks[T.root]
    near = [c for c in ranks if c != root and topo.may_write(root, c) and topo.may_write(c, root)]
    far = [c for c in ranks if c != root and c not in near]
    gate, deal = {}, {}
    for s in far:
        gate[s] = [w for w in near if topo.chip(w) == topo.chip(s) and topo.may_write(s, w)
                   and topo.rack(topo.host(w)) != topo.rack(topo.host(s))][0]
        w = topo.CORES_PER_CHIP
        chipc = [c for c in range(max(0, s - w), s + w) if topo.host(c) == topo.host(s) and topo.chip(c) == topo.chip(s)
                 and topo.may_write(c, gate[s])]
        par = chipc.index(s) % 2
        kc = [s] + [c for i, c in enumerate(chipc) if i % 2 == par and c != s]
        vc = [c for i, c in enumerate(chipc) if i % 2 != par]
        deal[s] = (kc[:KB], vc[:KB])
    gates = [gate[s] for s in far]
    return root, gates + [c for c in near if c not in gates], gate, deal


def rank_program(g, core, T, topo):
    root, near, gate, deal = _plan(T, topo)
    sem = T.sem
    far = list(gate)

    if core in gate:
        d = gate[core]
        kc, vc = deal[core]
        off = topo.mask(core, d)
        on = _bits(topo.mask(core, kc[1]))
        up = [e for e in on if not e & off]
        for b in range(KB):
            g.vector.memset(T.vaug0[:, b, 128:VW], 1.0).then_inc(sem.pad, 1)
        g.sync.dma_start(T.k_sb0[:, :], T.k[:, :]).then_inc(sem.kin, 16)
        g.sync.dma_start(T.vaug0[:, :, 0:128], T.v[:, :]).then_inc(sem.vin, 16)
        h, qr = len(up) // 2, len(up) // 4
        km = [None, sum(up[0:h]), sum(up[h:h + qr]), sum(up[h + qr:h + 2 * qr])]
        tr = []
        for b in range(1, KB):
            rid, pid = topo.addr(kc[b], core)
            tr.append(RemoteDMATransfer(dst_ids=[DstId(rid=rid, pnc=pid)], dma_engine_mask=km[b], remote_sem=sem.pin,
                                        src=T.k_sb0[:, 128 * b:128 * b + 128], dst=T.k_sb0[:, 128 * b:128 * b + 128]))
        g.wait_ge(sem.kin, 16)
        g.remote_dma_fused(tr, local_sem=sem.snt)
        rid, pid = topo.addr(d, core)
        g.remote_dma(T.k_sb1[:, 0:128], T.k_sb0[:, 0:128], sem.kb0, sem.snt, pid, rid, off)
        n4 = len(on) // KB
        tr = []
        for b in range(KB):
            rid, pid = topo.addr(vc[b], core)
            tr.append(RemoteDMATransfer(dst_ids=[DstId(rid=rid, pnc=pid)], dma_engine_mask=sum(on[n4 * b:n4 * b + n4]),
                                        remote_sem=sem.pin, src=T.vaug0[:, b, :], dst=T.vaug0[:, b, :]))
        g.wait_ge(sem.vin, 16)
        g.wait_ge(sem.pad, KB)
        g.remote_dma_fused(tr, local_sem=sem.snt)
        g.wait_ge(sem.snt, sum(_engines(x) for x in km[1:]) + _engines(off) + n4 * KB)
        return
    for s in far:
        kc, vc = deal[s]
        if core in kc or core in vc:
            d = gate[s]
            rid, pid = topo.addr(d, core)
            m = topo.mask(core, d)
            on = _bits(topo.mask(s, core))
            up = [e for e in on if not e & topo.mask(s, d)]
            if core in kc:
                b = kc.index(core)
                g.wait_ge(sem.pin, len(up) // 2 if b == 1 else len(up) // 4)
                g.remote_dma(T.k_sb1[:, 128 * b:128 * b + 128], T.k_sb0[:, 128 * b:128 * b + 128], sem["kb%d" % b], sem.snt,
                             pid, rid, m)
            else:
                b = vc.index(core)
                g.wait_ge(sem.pin, len(on) // KB)
                g.remote_dma(T.vaug1[:, b, :], T.vaug0[:, b, :], sem["vb%d" % b], sem.snt, pid, rid, m)
            g.wait_ge(sem.snt, _engines(m))
            return
    if core != root and core not in near:
        return

    is_root = core == root
    S = [T.S0, T.S1, T.S2, T.S3]
    qmask = topo.mask(root, near[0])
    for d in near:
        qmask &= topo.mask(root, d)

    if is_root:
        g.sync.dma_start(T.q_sb[:, :], T.q[:, :]).then_inc(sem.qin, 16)
    g.sync.dma_start(T.k_sb0[:, :], T.k[:, :]).then_inc(sem.kin, 16)
    g.sync.dma_start(T.vaug0[:, :, 0:128], T.v[:, :]).then_inc(sem.vin, 16)

    if is_root:
        g.wait_ge(sem.qin, 16)
        ids = []
        for d in near:
            rid, pid = topo.addr(d, core)
            ids.append(DstId(rid=rid, pnc=pid))
        g.remote_dma_fused([RemoteDMATransfer(dst_ids=ids, dma_engine_mask=qmask, remote_sem=sem.qin,
                                              srcs=[T.q_sb[:, :]], dsts=[T.q_sb[:, :] for _ in near], alu_op=0)],
                           local_sem=sem.snt)
    g.vector.memset(T.zeros[:, :], 0.0).then_inc(sem.zz, 1)
    for b in range(KB):
        g.vector.memset(T.vaug0[:, b, 128:VW], 1.0).then_inc(sem.pad, 1)
    g.scalar.wait_ge(sem.zz, 1)
    g.scalar.activation(T.ones[:, :], T.zeros[:, :], ActivationFunctionType.Exp).then_inc(sem.one, 1)
    g.wait_ge(sem.one, 1)
    g.affine_select(T.ident[:, :], T.ones[:, :], [[-1, 128]], AluOpType.is_equal, 0.0, 0, 1).then_inc(sem.idn, 1)
    g.tensor.wait_ge(sem.qin, 16 if is_root else _engines(qmask))
    g.tensor.wait_ge(sem.idn, 1)
    g.tensor.wait_ge(sem.pad, KB)

    groups = [(0, None if is_root else near.index(core), None)]
    for s in far:
        if gate[s] == core:
            groups.append((1, len(near) + far.index(s), s))
    if not is_root:
        rid, pid = topo.addr(root, core)
        m = topo.mask(core, root)

    for i, slot, s in groups:
        k_sb, vaug = (T.k_sb0, T.vaug0) if i == 0 else (T.k_sb1, T.vaug1)
        own = NP - 1 + i
        c0 = 512 * i

        def sm(n, b=None):
            return sem["%s%d" % (n, i)] if b is None else sem["%s%d%d" % (n, i, b)]
        for b in range(KB):
            if s is None:
                g.tensor.wait_ge(sem.kin, 16)
            else:
                g.tensor.wait_ge(sem["kb%d" % b], _engines(topo.mask(deal[s][0][b], core)))
            g.tensor.matmul(S[b][:, 0:128], T.q_sb[:, :], k_sb[:, 128 * b:128 * b + 128], True, True).then_inc(sm("s", b), 1)
        for b in range(KB):
            g.vector.wait_ge(sm("s", b), 1)
            g.vector.tensor_reduce(T.mx[:, 4 * i + b:4 * i + b + 1], S[b][:, 0:128], AxisListType.X,
                                   AluOpType.max).then_inc(sm("r"), 1)
        g.vector.wait_ge(sm("r"), KB)
        g.vector.tensor_reduce(T.nland[:, own:own + 1], T.mx[:, 4 * i:4 * i + KB], AxisListType.X, AluOpType.max,
                               negate=True).then_inc(sm("nm"), 1)
        g.scalar.wait_ge(sm("nm"), 1)
        for b in range(KB):
            g.scalar.activation(T.pw[:, c0 + 128 * b:c0 + 128 * b + 128], S[b][:, 0:128], ActivationFunctionType.Exp,
                                bias=T.nland[:, own:own + 1], scale=1.0).then_inc(sm("p", b), 1)
        for b in range(KB):
            g.tensor.wait_ge(sm("p", b), 1)
            g.tensor.matmul(S[b][:, 128:256], T.pw[:, c0 + 128 * b:c0 + 128 * b + 128], T.ident[:, :], True,
                            True).then_inc(sm("t", b), 1)
        for b in range(KB):
            g.vector.wait_ge(sm("t", b), 1)
            g.vector.tensor_copy(T.pt[:, c0 + 128 * b:c0 + 128 * b + 128], S[b][:, 128:256]).then_inc(sm("c", b), 1)
        if i > 0:
            g.tensor.wait_ge(sem.od0, 1)
        for b in range(KB):
            if s is None:
                g.tensor.wait_ge(sem.vin, 16)
            else:
                g.tensor.wait_ge(sem["vb%d" % b], _engines(topo.mask(deal[s][1][b], core)))
            g.tensor.wait_ge(sm("c", b), 1)
            mm = g.tensor.matmul(T.O[:, 0:OW], T.pt[:, c0 + 128 * b:c0 + 128 * b + 128], vaug[:, b, 0:OW], b == 0, b == KB - 1)
            if b == KB - 1:
                mm.then_inc(sm("pv"), 1)
        g.vector.wait_ge(sm("pv"), 1)
        g.vector.tensor_copy(T.oland[:, own, 0:OW], T.O[:, 0:OW]).then_inc(sm("od"), 1)
        if not is_root:
            g.wait_ge(sm("nm"), 1)
            g.remote_dma(T.nland[:, slot:slot + 1], T.nland[:, own:own + 1], sem.na, sem.snt, pid, rid, m)
            g.wait_ge(sm("od"), 1)
            g.remote_dma(T.oland[:, slot, 0:OW], T.oland[:, own, 0:OW], sem["oa%d" % slot], sem.snt, pid, rid, m)
    if not is_root:
        g.wait_ge(sem.snt, 2 * len(groups) * _engines(m))
        return

    own = NP - 1
    sender = near + [gate[s] for s in far]
    g.vector.wait_ge(sem.na, sum(_engines(topo.mask(w, root)) for w in sender))
    g.vector.wait_ge(sem.nm0, 1)
    g.vector.tensor_reduce(T.mn[:, 0:1], T.nland[:, 0:NP], AxisListType.X, AluOpType.min).then_inc(sem.mn, 1)
    g.scalar.wait_ge(sem.mn, 1)
    g.scalar.activation(T.ew[:, 0:NP], T.nland[:, 0:NP], ActivationFunctionType.Exp,
                        bias=T.mn[:, 0:1], scale=-1.0).then_inc(sem.ee, 1)
    order = [own] + list(range(len(sender)))
    g.vector.wait_ge(sem.ee, 1)
    g.vector.wait_ge(sem.idn, 1)
    for j in order:
        g.vector.tensor_scalar(T.dg[:, 128 * j:128 * j + 128], T.ident[:, :], T.ew[:, j:j + 1], None,
                               AluOpType.mult).then_inc(sem["d%d" % j], 1)
    for i, j in enumerate(order):
        g.tensor.wait_ge(sem["d%d" % j], 1)
        if j == own:
            g.tensor.wait_ge(sem.od0, 1)
        else:
            g.tensor.wait_ge(sem["oa%d" % j], _engines(topo.mask(sender[j], root)))
        mm = g.tensor.matmul(T.Y[:, 0:OW], T.dg[:, 128 * j:128 * j + 128], T.oland[:, j, 0:OW], i == 0, i == len(order) - 1)
        if i == len(order) - 1:
            mm.then_inc(sem.yy, 1)
    g.vector.wait_ge(sem.yy, 1)
    g.vector.reciprocal(T.rc[:, 0:1], T.Y[:, 128:129]).then_inc(sem.rcp, 1)
    g.vector.wait_ge(sem.rcp, 1)
    g.vector.tensor_scalar(T.ysb[:, :], T.Y[:, 0:128], T.rc[:, 0:1], None, AluOpType.mult).then_inc(sem.ys, 1)
    g.sync.wait_ge(sem.ys, 1)
    g.sync.dma_start(T.y[:, :], T.ysb[:, :]).then_inc(sem.st, 16)
    g.sync.wait_ge(sem.st, 16)
    g.wait_ge(sem.snt, _engines(qmask))
